import numpy as np
import ml_dtypes


def mxq(x, axis, fmt="e4m3"):
    dtype, down = {"e4m3": (ml_dtypes.float8_e4m3fn, 7), "e5m2": (ml_dtypes.float8_e5m2, 14)}[fmt]
    v = np.moveaxis(np.asarray(x, np.float32).astype(ml_dtypes.bfloat16).astype(np.float64), axis, -1)
    blocks = v.reshape(v.shape[:-1] + (-1, 32))
    amax = np.abs(blocks).max(-1, keepdims=True)
    byte = np.maximum(np.where(amax > 0, np.frexp(amax)[1] - 1 + 127, 0) - down, 1)
    scale = np.exp2(byte - 127.0)
    codes = (blocks / scale).astype(np.float32).astype(dtype).astype(np.float64)
    return np.moveaxis((codes * scale).reshape(v.shape), -1, axis)


WIDE = False


def mx_kscale(k):
    if not WIDE:
        return np.ones(k)
    levels = np.array([10, -10, 5, -5, 0])
    if k % 512:
        return np.exp2(np.random.permutation(np.resize(levels, k // 32))).repeat(32)
    a = np.empty((k // 512, 16))
    for p in range(k // 512):
        a[p, :8] = np.random.permutation(np.resize(levels, 8))
        for g in range(8):
            far = levels[np.abs(levels - a[p, g]) >= 10]
            a[p, g + 8] = far[np.random.randint(len(far))]
    return np.exp2(a.ravel()).repeat(32)


def f64(x):
    return np.asarray(x).astype(np.float64)


def striped8(idx):
    return np.asarray(idx).reshape(8, -1, 16).transpose(0, 2, 1).reshape(128, -1).astype(np.uint16)


def unstriped8(offs):
    return offs.reshape(8, 16, -1).transpose(0, 2, 1).reshape(8, -1).astype(np.int64)


def pick8(x, idx, run):
    r = np.arange(len(x))
    return x[r[:, None], idx[r % (8 * run) // run]]


E2M1 = np.array([0.0, 0.5, 1.0, 1.5, 2.0, 3.0, 4.0, 6.0, -0.0, -0.5, -1.0, -1.5, -2.0, -3.0, -4.0, -6.0])


def pack_weight(w, fmt):
    k, n = w.shape
    w = f64(np.asarray(w, np.float32).astype(ml_dtypes.bfloat16)).reshape(k // 32, 32, n)
    amax = np.abs(w).max(1)
    if fmt == "e4m3":
        byte = np.frexp(amax)[1] - 1 + 127 - 7
    else:
        mant, ex = np.frexp(amax / 6.0)
        byte = np.where(mant > 0.5, ex, ex - 1) + 127
    byte = np.clip(np.where(amax > 0, byte, 1), 1, 254)
    scaled = (w * np.exp2(127.0 - byte)[:, None, :]).reshape(k, n).astype(np.float32)
    by_word = np.ascontiguousarray(scaled.reshape(k // 512, 128, 4, n).transpose(0, 1, 3, 2))
    if fmt == "e4m3":
        words = by_word.astype(ml_dtypes.float8_e4m3fn).view(np.uint8)
    else:
        c = by_word.astype(ml_dtypes.float4_e2m1fn).view(np.uint8) & 0xF
        words = (c[..., 0::2] | (c[..., 1::2] << 4)).reshape(k // 512, 128, 2 * n)
    return np.ascontiguousarray(words), np.ascontiguousarray(byte.astype(np.uint8).reshape(k // 512, 16, n))


def unpack_weight(words, scales, fmt):
    g, _, n = scales.shape
    words = np.ascontiguousarray(words).reshape(g, 128, n, -1)
    if fmt == "e4m3":
        vals = words.view(ml_dtypes.float8_e4m3fn).astype(np.float64)
    else:
        nib = np.empty((g, 128, n, 4), np.uint8)
        nib[..., 0::2] = words & 0xF
        nib[..., 1::2] = words >> 4
        vals = E2M1[nib]
    vals = vals * np.repeat(np.exp2(scales.astype(np.float64) - 127.0), 8, axis=1)[..., None]
    return vals.transpose(0, 1, 3, 2).reshape(g * 512, n)


D, T, I, Q = 512, 1024, 512, 128


def setup_inputs():
    n = np.random.standard_normal
    idx = np.stack([np.random.permutation(T)[:I] for _ in range(8)])
    idx2 = np.stack([np.random.permutation(T)[:I] for _ in range(8)])
    idx3 = np.stack([np.random.permutation(T)[:I] for _ in range(8)])
    fd = mx_kscale(D)
    keysp = pack_weight(n((D, T)) / fd[:, None], "e2m1")
    return {
        "query": (n((D, Q)) * 0.9 / np.sqrt(D) * fd[:, None]).astype(np.float32),
        "query2": (n((D, Q)) * 0.9 / np.sqrt(D) * fd[:, None]).astype(np.float32),
        "keys_words": keysp[0],
        "keys_scales": keysp[1],
        "lam": (np.random.uniform(0.5, 1.5, (Q, 1))).astype(np.float32),
        "old": (1.0 * n((Q, T))).astype(np.float32),
        "offs": striped8(idx),
        "offs2": striped8(idx2),
        "offs3": striped8(idx3),
    }


def reference(query, query2, keys_words, keys_scales, lam, old, offs, offs2, offs3):
    idx = unstriped8(offs)
    idx2 = unstriped8(offs2)
    idx3 = unstriped8(offs3)
    keysu = unpack_weight(keys_words, keys_scales, "e2m1")
    queryq = mxq(f64(query), 0, "e4m3")
    a = queryq.T @ keysu
    query2q = mxq(f64(query2), 0, "e4m3")
    b = query2q.T @ keysu
    w = pick8(a, idx, 16) + pick8(a, idx2, 16) * np.tanh(pick8(b, idx, 16)) * f64(lam)
    f1 = np.zeros((Q, T))
    f1[np.arange(Q)[:, None], idx3[np.arange(Q) % 128 // 16]] = w
    y = np.maximum(f1, f64(old)) + f64(old) * 0.25
    return y

@@ -1,0 +1,140 @@
+from contextlib import ExitStack
+
+import concourse.mybir as mybir
+
+D, T, I, Q = 512, 1024, 512, 128
+FLOPS = 2 * 2 * D * T * Q
+
+F32 = mybir.dt.float32
+BF16 = mybir.dt.bfloat16
+I32 = mybir.dt.int32
+U32 = mybir.dt.uint32
+U16 = mybir.dt.uint16
+U8 = mybir.dt.uint8
+FP8X4 = mybir.dt.float8_e4m3fn_x4
+FP4X4 = mybir.dt.float4_e2m1fn_x4
+ALU = mybir.AluOpType
+ACT = mybir.ActivationFunctionType
+
+P = 128
+PACK = 4
+BANK = 512
+HALF = I // 2
+LIST_COLS = HALF // 16
+OUT_COLS = 256
+
+
+def tile_attend_turnedby_lean_largerput_heads_kernel(
+    tc, query, query2, keys_words, keys_scales, lam, old, offs, offs2, offs3, out
+):
+    nc = tc.nc
+    with ExitStack() as ctx:
+        keep = ctx.enter_context(tc.tile_pool(name="keep", bufs=1))
+        psum = ctx.enter_context(tc.psum_pool(name="psum", bufs=1))
+
+        lam_col = keep.tile([P, 1], F32, name="lam_col")
+        nc.gpsimd.dma_start(out=lam_col[:], in_=lam)
+        key_scales = keep.tile([P, T], U8, align_bytes=64, name="key_scales")
+        nc.vector.memset(key_scales[:].bitcast(I32), 0)
+        placed = keep.tile([P, T], F32, name="placed")
+        nc.vector.memset(placed[:], 0.0)
+
+        raw_a = keep.tile([P, PACK, Q], F32, name="raw_a")
+        nc.sync.dma_start(out=raw_a[:], in_=query.rearrange("(p j) q -> p j q", j=PACK))
+        key_words = keep.tile([P, 2 * T], U8, align_bytes=64, name="key_words")
+        nc.sync.dma_start(out=key_words[:].bitcast(I32), in_=keys_words[0].bitcast(I32))
+        for quad in range(4):
+            nc.sync.dma_start(
+                out=key_scales[32 * quad : 32 * quad + 4, :].bitcast(I32),
+                in_=keys_scales[0, 4 * quad : 4 * quad + 4, :].bitcast(I32),
+            )
+        raw_b = keep.tile([P, PACK, Q], F32, name="raw_b")
+        nc.sync.dma_start(out=raw_b[:], in_=query2.rearrange("(p j) q -> p j q", j=PACK))
+        idx2 = keep.tile([P, I // 16], U16, name="idx2")
+        nc.sync.dma_start(idx2[:], offs2)
+        idx = keep.tile([P, I // 16], U16, name="idx")
+        nc.sync.dma_start(idx[:], offs)
+        idx3 = keep.tile([P, I // 16], U16, name="idx3")
+        nc.sync.dma_start(idx3[:], offs3)
+        totals = keep.tile([P, T], F32, name="totals")
+        nc.sync.dma_start(out=totals[:], in_=old)
+
+        two_lam = keep.tile([P, I], F32, name="two_lam")
+        nc.scalar.activation(two_lam[:], lam_col[:].to_broadcast([P, I]), ACT.Copy, scale=2.0)
+
+        def quantise(raw, name):
+            grouped = keep.tile([P, Q, PACK], BF16, align_bytes=64, name=name + "_grouped")
+            nc.vector.tensor_copy(
+                out=grouped[:].rearrange("p (c i) j -> p c j i", i=4),
+                in_=raw[:].rearrange("p j (c i) -> p c j i", i=4),
+            )
+            codes = keep.tile([P, Q], U32, align_bytes=64, name=name + "_codes")
+            scales = keep.tile([P, Q], U8, align_bytes=64, name=name + "_scales")
+            nc.vector.quantize_mx(
+                out=codes[:].bitcast(FP8X4),
+                scales=scales[:],
+                in_=grouped[:].rearrange("p q j -> p (q j)"),
+            )
+            return codes, scales
+
+        def score(codes, scales, name, pieces):
+            whole = keep.tile([P, T], F32, name=name + "_whole")
+            t0 = 0
+            for width, copy_out in pieces:
+                bank = psum.tile([P, width], F32, name="%s_bank%d" % (name, t0))
+                nc.tensor.matmul_mx(
+                    out=bank[:],
+                    lhsT=codes[:].bitcast(FP8X4),
+                    lhsT_scale=scales[:],
+                    rhs=key_words[:, 2 * t0 : 2 * (t0 + width)].bitcast(FP4X4),
+                    rhs_scale=key_scales[:, t0 : t0 + width],
+                    start=True,
+                    stop=True,
+                )
+                copy_out(whole[:, t0 : t0 + width], bank[:])
+                t0 = t0 + width
+            return whole
+
+        on_scalar = nc.scalar.copy
+        codes_a, scales_a = quantise(raw_a, "a")
+        codes_b, scales_b = quantise(raw_b, "b")
+        a = score(codes_a, scales_a, "a", [(256, on_scalar)] * 4)
+        b = score(codes_b, scales_b, "b", [(256, on_scalar)] * 4)
+
+        second = keep.tile([P, I], F32, name="second")
+        nc.vector.tensor_tensor(second[:], a[:].indirect(idx2[:]), two_lam[:], ALU.mult)
+        lo, hi = slice(0, LIST_COLS), slice(LIST_COLS, 2 * LIST_COLS)
+        first0 = keep.tile([P, HALF], F32, name="first0")
+        nc.vector.tensor_copy(first0[:], a[:].indirect(idx[:, lo]))
+
+        sig0 = keep.tile([P, HALF], F32, name="sig0", tag="shared")
+        nc.scalar.activation(sig0[:], b[:].indirect(idx[:, lo]), ACT.Sigmoid, scale=2.0)
+        sig1 = keep.tile([P, HALF], F32, name="sig1")
+        nc.scalar.activation(sig1[:], b[:].indirect(idx[:, hi]), ACT.Sigmoid, scale=2.0)
+
+        turn0 = keep.tile([P, HALF], F32, name="turn0")
+        nc.vector.scalar_tensor_tensor(turn0[:], sig0[:], -0.5, second[:, :HALF], ALU.add, ALU.mult)
+        nc.vector.tensor_tensor(placed[:].indirect(idx3[:, lo]), turn0[:], first0[:], ALU.add)
+
+        first1 = keep.tile([P, HALF], F32, name="first1", tag="shared")
+        nc.scalar.activation(first1[:], a[:].indirect(idx[:, hi]), ACT.Copy)
+        turn1 = keep.tile([P, HALF], F32, name="turn1")
+        nc.vector.scalar_tensor_tensor(turn1[:], sig1[:], -0.5, second[:, HALF:], ALU.add, ALU.mult)
+        nc.vector.tensor_tensor(placed[:].indirect(idx3[:, hi]), turn1[:], first1[:], ALU.add)
+
+        larger = []
+        for c0 in range(0, T, OUT_COLS):
+            cols = slice(c0, c0 + OUT_COLS)
+            m = keep.tile([P, OUT_COLS], F32, name="larger%d" % c0)
+            nc.vector.tensor_tensor(m[:], placed[:, cols], totals[:, cols], ALU.max)
+            larger.append(m)
+            if len(larger) > 1:
+                finish(nc, keep, larger[-2], totals, out, c0 - OUT_COLS)
+        finish(nc, keep, larger[-1], totals, out, T - OUT_COLS)
+
+
+def finish(nc, keep, m, totals, out, c0):
+    cols = slice(c0, c0 + OUT_COLS)
+    result = keep.tile([P, OUT_COLS], F32, name="result%d" % c0)
+    nc.vector.scalar_tensor_tensor(result[:], totals[:, cols], 0.25, m[:], ALU.mult, ALU.add)
+    nc.sync.dma_start(out=out[:, cols], in_=result[:])

@@ -39,6 +39,11 @@ def tile_attend_turnedby_lean_largerput_heads_kernel(
         placed = keep.tile([P, T], F32, name="placed")
         nc.vector.memset(placed[:], 0.0)
 
+        warm_in = keep.tile([P, 1], F32, name="warm_in")
+        nc.gpsimd.memset(warm_in[:], 0.0)
+        warm_out = keep.tile([P, 1], F32, name="warm_out")
+        nc.scalar.activation(warm_out[:], warm_in[:], ACT.Sigmoid, scale=2.0)
+
         raw_a = keep.tile([P, PACK, Q], F32, name="raw_a")
         nc.sync.dma_start(out=raw_a[:], in_=query.rearrange("(p j) q -> p j q", j=PACK))
         key_words = keep.tile([P, 2 * T], U8, align_bytes=64, name="key_words")

@@ -1,6 +1,7 @@
 from contextlib import ExitStack
 
 import concourse.mybir as mybir
+from concourse.masks import make_identity
 
 D, T, I, Q = 512, 1024, 512, 128
 FLOPS = 2 * 2 * D * T * Q
@@ -21,7 +22,7 @@ PACK = 4
 BANK = 512
 HALF = I // 2
 LIST_COLS = HALF // 16
-OUT_COLS = 256
+BLOCKS = 2
 
 
 def tile_attend_turnedby_lean_largerput_heads_kernel(
@@ -33,7 +34,7 @@ def tile_attend_turnedby_lean_largerput_heads_kernel(
         psum = ctx.enter_context(tc.psum_pool(name="psum", bufs=1))
 
         lam_col = keep.tile([P, 1], F32, name="lam_col")
-        nc.gpsimd.dma_start(out=lam_col[:], in_=lam)
+        nc.scalar.dma_start(out=lam_col[:], in_=lam)
         key_scales = keep.tile([P, T], U8, align_bytes=64, name="key_scales")
         nc.vector.memset(key_scales[:].bitcast(I32), 0)
         placed = keep.tile([P, T], F32, name="placed")
@@ -44,14 +45,17 @@ def tile_attend_turnedby_lean_largerput_heads_kernel(
         warm_out = keep.tile([P, 1], F32, name="warm_out")
         nc.scalar.activation(warm_out[:], warm_in[:], ACT.Sigmoid, scale=2.0)
 
+        ident = keep.tile([P, P], F32, name="ident")
+        make_identity(nc, ident[:])
+
         raw_a = keep.tile([P, PACK, Q], F32, name="raw_a")
         nc.sync.dma_start(out=raw_a[:], in_=query.rearrange("(p j) q -> p j q", j=PACK))
         key_words = keep.tile([P, 2 * T], U8, align_bytes=64, name="key_words")
         nc.sync.dma_start(out=key_words[:].bitcast(I32), in_=keys_words[0].bitcast(I32))
-        for quad in range(4):
+        for r in range(4):
             nc.sync.dma_start(
-                out=key_scales[32 * quad : 32 * quad + 4, :].bitcast(I32),
-                in_=keys_scales[0, 4 * quad : 4 * quad + 4, :].bitcast(I32),
+                out=key_scales[r:P:32, :].bitcast(I32),
+                in_=keys_scales[0, r:16:4, :].bitcast(I32),
             )
         raw_b = keep.tile([P, PACK, Q], F32, name="raw_b")
         nc.sync.dma_start(out=raw_b[:], in_=query2.rearrange("(p j) q -> p j q", j=PACK))
@@ -64,8 +68,8 @@ def tile_attend_turnedby_lean_largerput_heads_kernel(
         totals = keep.tile([P, T], F32, name="totals")
         nc.sync.dma_start(out=totals[:], in_=old)
 
-        two_lam = keep.tile([P, I], F32, name="two_lam")
-        nc.scalar.activation(two_lam[:], lam_col[:].to_broadcast([P, I]), ACT.Copy, scale=2.0)
+        two_lam = keep.tile([P, HALF], F32, name="two_lam")
+        nc.scalar.activation(two_lam[:], lam_col[:].to_broadcast([P, HALF]), ACT.Copy, scale=2.0)
 
         def quantise(raw, name):
             grouped = keep.tile([P, Q, PACK], BF16, align_bytes=64, name=name + "_grouped")
@@ -85,8 +89,8 @@ def tile_attend_turnedby_lean_largerput_heads_kernel(
         def score(codes, scales, name, pieces):
             whole = keep.tile([P, T], F32, name=name + "_whole")
             t0 = 0
-            for width, copy_out in pieces:
-                bank = psum.tile([P, width], F32, name="%s_bank%d" % (name, t0))
+            for width, slot, copy_out in pieces:
+                bank = psum.tile([P, width], F32, name="%s_%d" % (name, t0), tag="bank%d" % slot)
                 nc.tensor.matmul_mx(
                     out=bank[:],
                     lhsT=codes[:].bitcast(FP8X4),
@@ -100,46 +104,79 @@ def tile_attend_turnedby_lean_largerput_heads_kernel(
                 t0 = t0 + width
             return whole
 
-        on_scalar = nc.scalar.copy
         codes_a, scales_a = quantise(raw_a, "a")
         codes_b, scales_b = quantise(raw_b, "b")
-        a = score(codes_a, scales_a, "a", [(256, on_scalar)] * 4)
-        b = score(codes_b, scales_b, "b", [(256, on_scalar)] * 4)
+        sc, ve = nc.scalar.copy, nc.vector.tensor_copy
+        a = score(codes_a, scales_a, "a", [(256, 0, sc), (256, 1, sc), (256, 2, sc), (256, 3, sc)])
+        b = score(codes_b, scales_b, "b", [(256, 4, sc), (256, 5, sc), (256, 6, sc), (128, 7, sc), (128, 0, sc)])
 
-        second = keep.tile([P, I], F32, name="second")
-        nc.vector.tensor_tensor(second[:], a[:].indirect(idx2[:]), two_lam[:], ALU.mult)
         lo, hi = slice(0, LIST_COLS), slice(LIST_COLS, 2 * LIST_COLS)
-        first0 = keep.tile([P, HALF], F32, name="first0")
+        second0 = keep.tile([P, HALF], F32, name="second0", tag="after_turn_a")
+        nc.vector.tensor_tensor(second0[:], a[:].indirect(idx2[:, lo]), two_lam[:], ALU.mult)
+        first0 = keep.tile([P, HALF], F32, name="first0", tag="after0a")
         nc.vector.tensor_copy(first0[:], a[:].indirect(idx[:, lo]))
+        second1 = keep.tile([P, HALF], F32, name="second1")
+        nc.vector.tensor_tensor(second1[:], a[:].indirect(idx2[:, hi]), two_lam[:], ALU.mult)
 
-        sig0 = keep.tile([P, HALF], F32, name="sig0", tag="shared")
+        sig0 = keep.tile([P, HALF], F32, name="sig0", tag="after_turn_b")
         nc.scalar.activation(sig0[:], b[:].indirect(idx[:, lo]), ACT.Sigmoid, scale=2.0)
-        sig1 = keep.tile([P, HALF], F32, name="sig1")
-        nc.scalar.activation(sig1[:], b[:].indirect(idx[:, hi]), ACT.Sigmoid, scale=2.0)
-
-        turn0 = keep.tile([P, HALF], F32, name="turn0")
-        nc.vector.scalar_tensor_tensor(turn0[:], sig0[:], -0.5, second[:, :HALF], ALU.add, ALU.mult)
+        turn0 = keep.tile([P, HALF], F32, name="turn0", tag="after0b")
+        nc.vector.scalar_tensor_tensor(turn0[:], sig0[:], -0.5, second0[:], ALU.add, ALU.mult)
         nc.vector.tensor_tensor(placed[:].indirect(idx3[:, lo]), turn0[:], first0[:], ALU.add)
 
-        first1 = keep.tile([P, HALF], F32, name="first1", tag="shared")
+        sig1 = keep.tile([P, HALF], F32, name="sig1", tag="after_turn_b")
+        nc.scalar.activation(sig1[:], b[:].indirect(idx[:, hi]), ACT.Sigmoid, scale=2.0)
+        first1 = keep.tile([P, HALF], F32, name="first1", tag="after_turn_a")
         nc.scalar.activation(first1[:], a[:].indirect(idx[:, hi]), ACT.Copy)
         turn1 = keep.tile([P, HALF], F32, name="turn1")
-        nc.vector.scalar_tensor_tensor(turn1[:], sig1[:], -0.5, second[:, HALF:], ALU.add, ALU.mult)
+        nc.vector.scalar_tensor_tensor(turn1[:], sig1[:], -0.5, second1[:], ALU.add, ALU.mult)
         nc.vector.tensor_tensor(placed[:].indirect(idx3[:, hi]), turn1[:], first1[:], ALU.add)
 
-        larger = []
-        for c0 in range(0, T, OUT_COLS):
-            cols = slice(c0, c0 + OUT_COLS)
-            m = keep.tile([P, OUT_COLS], F32, name="larger%d" % c0)
+        split = T - BLOCKS * P
+        blocks = [slice(split + k * P, split + (k + 1) * P) for k in range(BLOCKS)]
+        local = [slice(k * P, (k + 1) * P) for k in range(BLOCKS)]
+
+        def turn_add(bank, source, opens):
+            nc.tensor.matmul(bank, source, ident[:], start=opens, stop=not opens, is_transpose=True)
+
+        staged = psum.tile([P, BLOCKS * P], F32, name="staged", tag="bank0")
+        for k in range(BLOCKS):
+            nc.tensor.transpose(staged[:, local[k]], totals[:, blocks[k]], ident[:])
+        minus = keep.tile([P, BLOCKS * P], F32, name="minus", tag="after0b")
+        nc.scalar.activation(minus[:], totals[:, split:], ACT.Copy, scale=-1.0)
+        base_t = keep.tile([P, BLOCKS * P], F32, name="base_t", tag="after0a")
+        nc.scalar.activation(base_t[:], staged[:], ACT.Copy, scale=1.25)
+        diff = [psum.tile([P, P], F32, name="diff%d" % k, tag="bank%d" % (1 + k)) for k in range(BLOCKS)]
+        total = [psum.tile([P, P], F32, name="total%d" % k, tag="bank%d" % ((1 + BLOCKS + k) % 8)) for k in range(BLOCKS)]
+        for k in range(BLOCKS):
+            turn_add(diff[k][:], minus[:, local[k]], True)
+        for k in range(BLOCKS):
+            turn_add(total[k][:], base_t[:, local[k]], True)
+        for k in range(BLOCKS):
+            turn_add(diff[k][:], placed[:, blocks[k]], False)
+        for k in range(BLOCKS):
+            excess = keep.tile([P, P], F32, name="excess%d" % k)
+            nc.scalar.activation(excess[:], diff[k][:], ACT.Relu)
+            turn_add(total[k][:], excess[:], False)
+        tail = keep.tile([P, BLOCKS * P], F32, name="tail")
+        for k in range(BLOCKS):
+            nc.scalar.copy(tail[:, local[k]], total[k][:])
+        nc.scalar.dma_start(out=out[:, split:], in_=tail[:])
+
+        pieces = [slice(0, 256), slice(256, 512), slice(512, split)]
+        def larger_of(cols):
+            m = keep.tile([P, cols.stop - cols.start], F32, name="larger%d" % cols.start)
             nc.vector.tensor_tensor(m[:], placed[:, cols], totals[:, cols], ALU.max)
-            larger.append(m)
-            if len(larger) > 1:
-                finish(nc, keep, larger[-2], totals, out, c0 - OUT_COLS)
-        finish(nc, keep, larger[-1], totals, out, T - OUT_COLS)
+            return m
 
+        def finish(cols, m):
+            result = keep.tile([P, cols.stop - cols.start], F32, name="result%d" % cols.start)
+            nc.vector.scalar_tensor_tensor(result[:], totals[:, cols], 0.25, m[:], ALU.mult, ALU.add)
+            nc.sync.dma_start(out=out[:, cols], in_=result[:])
 
-def finish(nc, keep, m, totals, out, c0):
-    cols = slice(c0, c0 + OUT_COLS)
-    result = keep.tile([P, OUT_COLS], F32, name="result%d" % c0)
-    nc.vector.scalar_tensor_tensor(result[:], totals[:, cols], 0.25, m[:], ALU.mult, ALU.add)
-    nc.sync.dma_start(out=out[:, cols], in_=result[:])
+        waiting = larger_of(pieces[0])
+        for before, cols in zip(pieces, pieces[1:]):
+            m = larger_of(cols)
+            finish(before, waiting)
+            waiting = m
+        finish(pieces[-1], waiting)

@@ -19,9 +19,11 @@ ACT = mybir.ActivationFunctionType
 
 P = 128
 PACK = 4
-BANK = 512
+QUADRANT = 32
+SCALE_ROWS = D // 32
 HALF = I // 2
 LIST_COLS = HALF // 16
+PIECE = 256
 BLOCKS = 2
 
 
@@ -34,7 +36,8 @@ def tile_attend_turnedby_lean_largerput_heads_kernel(
         psum = ctx.enter_context(tc.psum_pool(name="psum", bufs=1))
 
         lam_col = keep.tile([P, 1], F32, name="lam_col")
-        nc.scalar.dma_start(out=lam_col[:], in_=lam)
+        nc.gpsimd.dma_start(out=lam_col[:], in_=lam)
+
         key_scales = keep.tile([P, T], U8, align_bytes=64, name="key_scales")
         nc.vector.memset(key_scales[:].bitcast(I32), 0)
         placed = keep.tile([P, T], F32, name="placed")
@@ -54,8 +57,8 @@ def tile_attend_turnedby_lean_largerput_heads_kernel(
         nc.sync.dma_start(out=key_words[:].bitcast(I32), in_=keys_words[0].bitcast(I32))
         for r in range(4):
             nc.sync.dma_start(
-                out=key_scales[r:P:32, :].bitcast(I32),
-                in_=keys_scales[0, r:16:4, :].bitcast(I32),
+                out=key_scales[r:P:QUADRANT, :].bitcast(I32),
+                in_=keys_scales[0, r:SCALE_ROWS:4, :].bitcast(I32),
             )
         raw_b = keep.tile([P, PACK, Q], F32, name="raw_b")
         nc.sync.dma_start(out=raw_b[:], in_=query2.rearrange("(p j) q -> p j q", j=PACK))
@@ -68,11 +71,8 @@ def tile_attend_turnedby_lean_largerput_heads_kernel(
         totals = keep.tile([P, T], F32, name="totals")
         nc.sync.dma_start(out=totals[:], in_=old)
 
-        two_lam = keep.tile([P, HALF], F32, name="two_lam")
-        nc.scalar.activation(two_lam[:], lam_col[:].to_broadcast([P, HALF]), ACT.Copy, scale=2.0)
-
         def quantise(raw, name):
-            grouped = keep.tile([P, Q, PACK], BF16, align_bytes=64, name=name + "_grouped")
+            grouped = keep.tile([P, Q, PACK], BF16, align_bytes=64, name=name + "_grouped", tag=name + "_grouped")
             nc.vector.tensor_copy(
                 out=grouped[:].rearrange("p (c i) j -> p c j i", i=4),
                 in_=raw[:].rearrange("p j (c i) -> p c j i", i=4),
@@ -86,11 +86,11 @@ def tile_attend_turnedby_lean_largerput_heads_kernel(
             )
             return codes, scales
 
-        def score(codes, scales, name, pieces):
+        def score(codes, scales, name, passes):
             whole = keep.tile([P, T], F32, name=name + "_whole")
             t0 = 0
-            for width, slot, copy_out in pieces:
-                bank = psum.tile([P, width], F32, name="%s_%d" % (name, t0), tag="bank%d" % slot)
+            for width, bank_no in passes:
+                bank = psum.tile([P, width], F32, name="%s_%d" % (name, t0), tag="bank%d" % bank_no)
                 nc.tensor.matmul_mx(
                     out=bank[:],
                     lhsT=codes[:].bitcast(FP8X4),
@@ -100,15 +100,17 @@ def tile_attend_turnedby_lean_largerput_heads_kernel(
                     start=True,
                     stop=True,
                 )
-                copy_out(whole[:, t0 : t0 + width], bank[:])
+                nc.scalar.copy(whole[:, t0 : t0 + width], bank[:])
                 t0 = t0 + width
             return whole
 
         codes_a, scales_a = quantise(raw_a, "a")
         codes_b, scales_b = quantise(raw_b, "b")
-        sc, ve = nc.scalar.copy, nc.vector.tensor_copy
-        a = score(codes_a, scales_a, "a", [(256, 0, sc), (256, 1, sc), (256, 2, sc), (256, 3, sc)])
-        b = score(codes_b, scales_b, "b", [(256, 4, sc), (256, 5, sc), (256, 6, sc), (128, 7, sc), (128, 0, sc)])
+        two_lam = keep.tile([P, HALF], F32, align_bytes=64, name="two_lam", tag="b_grouped")
+        nc.vector.tensor_scalar(two_lam[:], lam_col[:].to_broadcast([P, HALF]), 2.0, None, ALU.mult)
+
+        a = score(codes_a, scales_a, "a", [(PIECE, k) for k in range(4)])
+        b = score(codes_b, scales_b, "b", [(PIECE, 4), (PIECE, 5), (PIECE, 6), (PIECE // 2, 7), (PIECE // 2, 0)])
 
         lo, hi = slice(0, LIST_COLS), slice(LIST_COLS, 2 * LIST_COLS)
         second0 = keep.tile([P, HALF], F32, name="second0", tag="after_turn_a")
@@ -147,7 +149,7 @@ def tile_attend_turnedby_lean_largerput_heads_kernel(
         base_t = keep.tile([P, BLOCKS * P], F32, name="base_t", tag="after0a")
         nc.scalar.activation(base_t[:], staged[:], ACT.Copy, scale=1.25)
         diff = [psum.tile([P, P], F32, name="diff%d" % k, tag="bank%d" % (1 + k)) for k in range(BLOCKS)]
-        total = [psum.tile([P, P], F32, name="total%d" % k, tag="bank%d" % ((1 + BLOCKS + k) % 8)) for k in range(BLOCKS)]
+        total = [psum.tile([P, P], F32, name="total%d" % k, tag="bank%d" % (1 + BLOCKS + k)) for k in range(BLOCKS)]
         for k in range(BLOCKS):
             turn_add(diff[k][:], minus[:, local[k]], True)
         for k in range(BLOCKS):
@@ -163,20 +165,21 @@ def tile_attend_turnedby_lean_largerput_heads_kernel(
             nc.scalar.copy(tail[:, local[k]], total[k][:])
         nc.scalar.dma_start(out=out[:, split:], in_=tail[:])
 
-        pieces = [slice(0, 256), slice(256, 512), slice(512, split)]
-        def larger_of(cols):
-            m = keep.tile([P, cols.stop - cols.start], F32, name="larger%d" % cols.start)
-            nc.vector.tensor_tensor(m[:], placed[:, cols], totals[:, cols], ALU.max)
-            return m
+        pieces = [slice(c0, c0 + PIECE) for c0 in range(0, split, PIECE)]
 
-        def finish(cols, m):
-            result = keep.tile([P, cols.stop - cols.start], F32, name="result%d" % cols.start)
-            nc.vector.scalar_tensor_tensor(result[:], totals[:, cols], 0.25, m[:], ALU.mult, ALU.add)
+        def larger_of(cols):
+            larger = keep.tile([P, PIECE], F32, name="larger%d" % cols.start)
+            nc.vector.tensor_tensor(larger[:], placed[:, cols], totals[:, cols], ALU.max)
+            return larger
+
+        def finish(cols, larger):
+            result = keep.tile([P, PIECE], F32, name="result%d" % cols.start)
+            nc.vector.scalar_tensor_tensor(result[:], totals[:, cols], 0.25, larger[:], ALU.mult, ALU.add)
             nc.sync.dma_start(out=out[:, cols], in_=result[:])
 
         waiting = larger_of(pieces[0])
         for before, cols in zip(pieces, pieces[1:]):
-            m = larger_of(cols)
+            larger = larger_of(cols)
             finish(before, waiting)
-            waiting = m
+            waiting = larger
         finish(pieces[-1], waiting)

from contextlib import ExitStack

import concourse.mybir as mybir
from concourse.masks import make_identity

D, T, I, Q = 512, 1024, 512, 128
FLOPS = 2 * 2 * D * T * Q

F32 = mybir.dt.float32
BF16 = mybir.dt.bfloat16
I32 = mybir.dt.int32
U32 = mybir.dt.uint32
U16 = mybir.dt.uint16
U8 = mybir.dt.uint8
FP8X4 = mybir.dt.float8_e4m3fn_x4
FP4X4 = mybir.dt.float4_e2m1fn_x4
ALU = mybir.AluOpType
ACT = mybir.ActivationFunctionType

P = 128
PACK = 4
QUADRANT = 32
SCALE_ROWS = D // 32
HALF = I // 2
LIST_COLS = HALF // 16
PIECE = 256
BLOCKS = 2


def tile_attend_turnedby_lean_largerput_heads_kernel(
    tc, query, query2, keys_words, keys_scales, lam, old, offs, offs2, offs3, out
):
    nc = tc.nc
    with ExitStack() as ctx:
        keep = ctx.enter_context(tc.tile_pool(name="keep", bufs=1))
        psum = ctx.enter_context(tc.psum_pool(name="psum", bufs=1))

        lam_col = keep.tile([P, 1], F32, name="lam_col")
        nc.gpsimd.dma_start(out=lam_col[:], in_=lam)

        key_scales = keep.tile([P, T], U8, align_bytes=64, name="key_scales")
        nc.vector.memset(key_scales[:].bitcast(I32), 0)
        placed = keep.tile([P, T], F32, name="placed")
        nc.vector.memset(placed[:], 0.0)

        warm_in = keep.tile([P, 1], F32, name="warm_in")
        nc.gpsimd.memset(warm_in[:], 0.0)
        warm_out = keep.tile([P, 1], F32, name="warm_out")
        nc.scalar.activation(warm_out[:], warm_in[:], ACT.Sigmoid, scale=2.0)

        ident = keep.tile([P, P], F32, name="ident")
        make_identity(nc, ident[:])

        raw_a = keep.tile([P, PACK, Q], F32, name="raw_a")
        nc.sync.dma_start(out=raw_a[:], in_=query.rearrange("(p j) q -> p j q", j=PACK))
        key_words = keep.tile([P, 2 * T], U8, align_bytes=64, name="key_words")
        nc.sync.dma_start(out=key_words[:].bitcast(I32), in_=keys_words[0].bitcast(I32))
        for r in range(4):
            nc.sync.dma_start(
                out=key_scales[r:P:QUADRANT, :].bitcast(I32),
                in_=keys_scales[0, r:SCALE_ROWS:4, :].bitcast(I32),
            )
        raw_b = keep.tile([P, PACK, Q], F32, name="raw_b")
        nc.sync.dma_start(out=raw_b[:], in_=query2.rearrange("(p j) q -> p j q", j=PACK))
        idx2 = keep.tile([P, I // 16], U16, name="idx2")
        nc.sync.dma_start(idx2[:], offs2)
        idx = keep.tile([P, I // 16], U16, name="idx")
        nc.sync.dma_start(idx[:], offs)
        idx3 = keep.tile([P, I // 16], U16, name="idx3")
        nc.sync.dma_start(idx3[:], offs3)
        totals = keep.tile([P, T], F32, name="totals")
        nc.sync.dma_start(out=totals[:], in_=old)

        def quantise(raw, name):
            grouped = keep.tile([P, Q, PACK], BF16, align_bytes=64, name=name + "_grouped", tag=name + "_grouped")
            nc.vector.tensor_copy(
                out=grouped[:].rearrange("p (c i) j -> p c j i", i=4),
                in_=raw[:].rearrange("p j (c i) -> p c j i", i=4),
            )
            codes = keep.tile([P, Q], U32, align_bytes=64, name=name + "_codes")
            scales = keep.tile([P, Q], U8, align_bytes=64, name=name + "_scales")
            nc.vector.quantize_mx(
                out=codes[:].bitcast(FP8X4),
                scales=scales[:],
                in_=grouped[:].rearrange("p q j -> p (q j)"),
            )
            return codes, scales

        def score(codes, scales, name, passes):
            whole = keep.tile([P, T], F32, name=name + "_whole")
            t0 = 0
            for width, bank_no in passes:
                bank = psum.tile([P, width], F32, name="%s_%d" % (name, t0), tag="bank%d" % bank_no)
                nc.tensor.matmul_mx(
                    out=bank[:],
                    lhsT=codes[:].bitcast(FP8X4),
                    lhsT_scale=scales[:],
                    rhs=key_words[:, 2 * t0 : 2 * (t0 + width)].bitcast(FP4X4),
                    rhs_scale=key_scales[:, t0 : t0 + width],
                    start=True,
                    stop=True,
                )
                nc.scalar.copy(whole[:, t0 : t0 + width], bank[:])
                t0 = t0 + width
            return whole

        codes_a, scales_a = quantise(raw_a, "a")
        codes_b, scales_b = quantise(raw_b, "b")
        two_lam = keep.tile([P, HALF], F32, align_bytes=64, name="two_lam", tag="b_grouped")
        nc.vector.tensor_scalar(two_lam[:], lam_col[:].to_broadcast([P, HALF]), 2.0, None, ALU.mult)

        a = score(codes_a, scales_a, "a", [(PIECE, k) for k in range(4)])
        b = score(codes_b, scales_b, "b", [(PIECE, 4), (PIECE, 5), (PIECE, 6), (PIECE // 2, 7), (PIECE // 2, 0)])

        lo, hi = slice(0, LIST_COLS), slice(LIST_COLS, 2 * LIST_COLS)
        second0 = keep.tile([P, HALF], F32, name="second0", tag="after_turn_a")
        nc.vector.tensor_tensor(second0[:], a[:].indirect(idx2[:, lo]), two_lam[:], ALU.mult)
        first0 = keep.tile([P, HALF], F32, name="first0", tag="after0a")
        nc.vector.tensor_copy(first0[:], a[:].indirect(idx[:, lo]))
        second1 = keep.tile([P, HALF], F32, name="second1")
        nc.vector.tensor_tensor(second1[:], a[:].indirect(idx2[:, hi]), two_lam[:], ALU.mult)

        sig0 = keep.tile([P, HALF], F32, name="sig0", tag="after_turn_b")
        nc.scalar.activation(sig0[:], b[:].indirect(idx[:, lo]), ACT.Sigmoid, scale=2.0)
        turn0 = keep.tile([P, HALF], F32, name="turn0", tag="after0b")
        nc.vector.scalar_tensor_tensor(turn0[:], sig0[:], -0.5, second0[:], ALU.add, ALU.mult)
        nc.vector.tensor_tensor(placed[:].indirect(idx3[:, lo]), turn0[:], first0[:], ALU.add)

        sig1 = keep.tile([P, HALF], F32, name="sig1", tag="after_turn_b")
        nc.scalar.activation(sig1[:], b[:].indirect(idx[:, hi]), ACT.Sigmoid, scale=2.0)
        first1 = keep.tile([P, HALF], F32, name="first1", tag="after_turn_a")
        nc.scalar.activation(first1[:], a[:].indirect(idx[:, hi]), ACT.Copy)
        turn1 = keep.tile([P, HALF], F32, name="turn1")
        nc.vector.scalar_tensor_tensor(turn1[:], sig1[:], -0.5, second1[:], ALU.add, ALU.mult)
        nc.vector.tensor_tensor(placed[:].indirect(idx3[:, hi]), turn1[:], first1[:], ALU.add)

        split = T - BLOCKS * P
        blocks = [slice(split + k * P, split + (k + 1) * P) for k in range(BLOCKS)]
        local = [slice(k * P, (k + 1) * P) for k in range(BLOCKS)]

        def turn_add(bank, source, opens):
            nc.tensor.matmul(bank, source, ident[:], start=opens, stop=not opens, is_transpose=True)

        staged = psum.tile([P, BLOCKS * P], F32, name="staged", tag="bank0")
        for k in range(BLOCKS):
            nc.tensor.transpose(staged[:, local[k]], totals[:, blocks[k]], ident[:])
        minus = keep.tile([P, BLOCKS * P], F32, name="minus", tag="after0b")
        nc.scalar.activation(minus[:], totals[:, split:], ACT.Copy, scale=-1.0)
        base_t = keep.tile([P, BLOCKS * P], F32, name="base_t", tag="after0a")
        nc.scalar.activation(base_t[:], staged[:], ACT.Copy, scale=1.25)
        diff = [psum.tile([P, P], F32, name="diff%d" % k, tag="bank%d" % (1 + k)) for k in range(BLOCKS)]
        total = [psum.tile([P, P], F32, name="total%d" % k, tag="bank%d" % (1 + BLOCKS + k)) for k in range(BLOCKS)]
        for k in range(BLOCKS):
            turn_add(diff[k][:], minus[:, local[k]], True)
        for k in range(BLOCKS):
            turn_add(total[k][:], base_t[:, local[k]], True)
        for k in range(BLOCKS):
            turn_add(diff[k][:], placed[:, blocks[k]], False)
        for k in range(BLOCKS):
            excess = keep.tile([P, P], F32, name="excess%d" % k)
            nc.scalar.activation(excess[:], diff[k][:], ACT.Relu)
            turn_add(total[k][:], excess[:], False)
        tail = keep.tile([P, BLOCKS * P], F32, name="tail")
        for k in range(BLOCKS):
            nc.scalar.copy(tail[:, local[k]], total[k][:])
        nc.scalar.dma_start(out=out[:, split:], in_=tail[:])

        pieces = [slice(c0, c0 + PIECE) for c0 in range(0, split, PIECE)]

        def larger_of(cols):
            larger = keep.tile([P, PIECE], F32, name="larger%d" % cols.start)
            nc.vector.tensor_tensor(larger[:], placed[:, cols], totals[:, cols], ALU.max)
            return larger

        def finish(cols, larger):
            result = keep.tile([P, PIECE], F32, name="result%d" % cols.start)
            nc.vector.scalar_tensor_tensor(result[:], totals[:, cols], 0.25, larger[:], ALU.mult, ALU.add)
            nc.sync.dma_start(out=out[:, cols], in_=result[:])

        waiting = larger_of(pieces[0])
        for before, cols in zip(pieces, pieces[1:]):
            larger = larger_of(cols)
            finish(before, waiting)
            waiting = larger
        finish(pieces[-1], waiting)
